import numpy as np
import ml_dtypes


def mxq(x, axis, fmt="e4m3"):
    dtype, down = {"e4m3": (ml_dtypes.float8_e4m3fn, 7), "e5m2": (ml_dtypes.float8_e5m2, 14)}[fmt]
    v = np.moveaxis(np.asarray(x, np.float32).astype(ml_dtypes.bfloat16).astype(np.float64), axis, -1)
    blocks = v.reshape(v.shape[:-1] + (-1, 32))
    amax = np.abs(blocks).max(-1, keepdims=True)
    byte = np.maximum(np.where(amax > 0, np.frexp(amax)[1] - 1 + 127, 0) - down, 1)
    scale = np.exp2(byte - 127.0)
    codes = (blocks / scale).astype(np.float32).astype(dtype).astype(np.float64)
    return np.moveaxis((codes * scale).reshape(v.shape), -1, axis)


WIDE = False


def mx_kscale(k):
    if not WIDE:
        return np.ones(k)
    levels = np.array([10, -10, 5, -5, 0])
    if k % 512:
        return np.exp2(np.random.permutation(np.resize(levels, k // 32))).repeat(32)
    a = np.empty((k // 512, 16))
    for p in range(k // 512):
        a[p, :8] = np.random.permutation(np.resize(levels, 8))
        for g in range(8):
            far = levels[np.abs(levels - a[p, g]) >= 10]
            a[p, g + 8] = far[np.random.randint(len(far))]
    return np.exp2(a.ravel()).repeat(32)


def f64(x):
    return np.asarray(x).astype(np.float64)


def striped(idx):
    return np.tile(idx.reshape(-1, 16).T, (8, 1)).astype(np.uint16)


def unstriped(offs):
    return offs[:16].T.reshape(-1).astype(np.int64)


E2M1 = np.array([0.0, 0.5, 1.0, 1.5, 2.0, 3.0, 4.0, 6.0, -0.0, -0.5, -1.0, -1.5, -2.0, -3.0, -4.0, -6.0])


def pack_weight(w, fmt):
    k, n = w.shape
    w = f64(np.asarray(w, np.float32).astype(ml_dtypes.bfloat16)).reshape(k // 32, 32, n)
    amax = np.abs(w).max(1)
    if fmt == "e4m3":
        byte = np.frexp(amax)[1] - 1 + 127 - 7
    else:
        mant, ex = np.frexp(amax / 6.0)
        byte = np.where(mant > 0.5, ex, ex - 1) + 127
    byte = np.clip(np.where(amax > 0, byte, 1), 1, 254)
    scaled = (w * np.exp2(127.0 - byte)[:, None, :]).reshape(k, n).astype(np.float32)
    by_word = np.ascontiguousarray(scaled.reshape(k // 512, 128, 4, n).transpose(0, 1, 3, 2))
    if fmt == "e4m3":
        words = by_word.astype(ml_dtypes.float8_e4m3fn).view(np.uint8)
    else:
        c = by_word.astype(ml_dtypes.float4_e2m1fn).view(np.uint8) & 0xF
        words = (c[..., 0::2] | (c[..., 1::2] << 4)).reshape(k // 512, 128, 2 * n)
    return np.ascontiguousarray(words), np.ascontiguousarray(byte.astype(np.uint8).reshape(k // 512, 16, n))


def unpack_weight(words, scales, fmt):
    g, _, n = scales.shape
    words = np.ascontiguousarray(words).reshape(g, 128, n, -1)
    if fmt == "e4m3":
        vals = words.view(ml_dtypes.float8_e4m3fn).astype(np.float64)
    else:
        nib = np.empty((g, 128, n, 4), np.uint8)
        nib[..., 0::2] = words & 0xF
        nib[..., 1::2] = words >> 4
        vals = E2M1[nib]
    vals = vals * np.repeat(np.exp2(scales.astype(np.float64) - 127.0), 8, axis=1)[..., None]
    return vals.transpose(0, 1, 3, 2).reshape(g * 512, n)


def gelu(v):
    return 0.5 * v * (1.0 + np.tanh(np.sqrt(2.0 / np.pi) * (v + 0.044715 * v**3)))


def often(T, S):
    return np.random.permutation(T)[(T * np.random.uniform(0, 1, S) ** 4).astype(np.int64)]


K, M, H, N, T, S, P = 512, 1024, 1024, 512, 2048, 1024, 512

def setup_inputs():
    n = np.random.standard_normal
    s1 = mx_kscale(K)[:, None]
    s2 = mx_kscale(M)[:, None]
    s3 = mx_kscale(K)[:, None]
    u = mx_kscale(H)[:, None]
    d = {}
    d["tab_words"], d["tab_scales"] = pack_weight(n((K, T)) * s1, "e4m3")
    d["tab2_words"], d["tab2_scales"] = pack_weight(n((M, T)) * s2, "e4m3")
    d["tab3_words"], d["tab3_scales"] = pack_weight(n((K, T)) * s3, "e4m3")
    d["offs"] = striped(np.random.permutation(T)[:S])
    d["offs2"] = striped(np.random.permutation(T)[:S])
    d["offs3"] = striped(np.random.permutation(T)[:S])
    d["pos1"] = striped(np.random.permutation(S)[:P])
    d["pos2"] = striped(often(S, P))
    d["pos3"] = striped(often(S, P))
    d["w1"] = (n((K, H)) / K ** 0.5 / s1 * u.T ** 0.5).astype(np.float32)
    d["w2_words"], d["w2_scales"] = pack_weight(n((M, H)) / M ** 0.5 / s2 * u.T ** 0.5, "e4m3")
    d["w3_words"], d["w3_scales"] = pack_weight(n((K, H)) / K ** 0.5 / s3 * u.T, "e2m1")
    d["cap"] = (np.random.uniform(1.0, 3.0, H) * u[:, 0]).astype(np.float32)
    d["w4"] = (n((H, N)) / H ** 0.5 / u).astype(np.float32)
    d["pref"] = n((N, P)).astype(np.float32)
    return d

def reference(tab_words, tab_scales, tab2_words, tab2_scales, tab3_words, tab3_scales, offs, offs2, offs3, pos1, pos2, pos3, w1, w2_words, w2_scales, w3_words, w3_scales, cap, w4, pref):
    v = unpack_weight(tab_words, tab_scales, "e4m3")[:, unstriped(offs)]
    v2 = unpack_weight(tab2_words, tab2_scales, "e4m3")[:, unstriped(offs2)]
    v3 = unpack_weight(tab3_words, tab3_scales, "e4m3")[:, unstriped(offs3)]
    a = mxq(f64(w1), 0, "e4m3").T @ v
    b = unpack_weight(w2_words, w2_scales, "e4m3").T @ v2
    d = unpack_weight(w3_words, w3_scales, "e2m1").T @ v3
    gap = a[:, unstriped(pos1)] - b[:, unstriped(pos2)]
    z = np.minimum(np.square(gap), f64(cap)[:, None]) - d[:, unstriped(pos3)]
    y = mxq(f64(w4), 0, "e4m3").T @ mxq(z, 0, "e4m3")
    return y + f64(pref)

@@ -1,0 +1,271 @@
+from contextlib import ExitStack
+
+import concourse.mybir as mybir
+
+K, M, H, N, T, S, J = 512, 1024, 1024, 512, 2048, 1024, 512
+FLOPS = 2 * H * S * (K + M + K) + 2 * H * N * J
+
+F32 = mybir.dt.float32
+BF16 = mybir.dt.bfloat16
+I32 = mybir.dt.int32
+U32 = mybir.dt.uint32
+U16 = mybir.dt.uint16
+U8 = mybir.dt.uint8
+FP8X4 = mybir.dt.float8_e4m3fn_x4
+FP4X4 = mybir.dt.float4_e2m1fn_x4
+ACT = mybir.ActivationFunctionType
+ALU = mybir.AluOpType
+
+P = 128
+BANK = 512
+HALF = 256
+
+
+def tile_list_key_blank_bench_kernel(
+    tc, tab_words, tab_scales, tab2_words, tab2_scales, tab3_words, tab3_scales,
+    offs, offs2, offs3, pos1, pos2, pos3,
+    w1, w2_words, w2_scales, w3_words, w3_scales, cap, w4, pref, out,
+):
+    nc = tc.nc
+    with ExitStack() as ctx:
+        keep = ctx.enter_context(tc.tile_pool(name="keep", bufs=1))
+        psum = ctx.enter_context(tc.psum_pool(name="psum", bufs=1))
+
+        def held(name, shape, dtype):
+            return keep.tile(shape, dtype, name=name, align_bytes=64)
+
+        def load_list(name, src):
+            dst = held(name, [P, src.shape[1]], U16)
+            nc.sync.dma_start(dst[:], src)
+            return dst
+
+        def load_scale_rows(dst, src):
+            rows = 4 * src.shape[0]
+            for q in range(4):
+                nc.sync.dma_start(dst[32 * q : 32 * q + rows, :].bitcast(I32), src[:, 4 * q : 4 * q + 4, :].bitcast(I32))
+
+        def load_words(name, src):
+            dst = held(name, [P, T], I32)
+            nc.sync.dma_start(dst[:], src.rearrange("p n i -> p (n i)").bitcast(I32))
+            return dst
+
+        tab_s = held("tab_s", [P, T], U8)
+        tab2_s = held("tab2_s", [P, T], U8)
+        tab3_s = held("tab3_s", [P, T], U8)
+        w_s_raw = held("w_s_raw", [P, 2 * H], U8)
+        for plane in (tab_s, tab2_s, tab3_s, w_s_raw):
+            nc.vector.memset(plane[:].bitcast(I32), 0)
+
+        idx = load_list("idx", offs)
+        idx2 = load_list("idx2", offs2)
+        idx3 = load_list("idx3", offs3)
+        load_scale_rows(tab_s, tab_scales)
+        tab_w = load_words("tab_w", tab_words[0])
+        load_scale_rows(tab2_s, tab2_scales)
+        w1_raw = []
+        for b in range(2):
+            raw = keep.tile([P, 4, BANK], F32, name="w1_raw", tag="w_raw", bufs=2, align_bytes=64)
+            nc.sync.dma_start(raw[:], w1[:, BANK * b : BANK * (b + 1)].rearrange("(p j) c -> p j c", j=4))
+            w1_raw.append(raw)
+        load_scale_rows(tab3_s, tab3_scales)
+        tab2_w = [load_words("tab2_w%d" % a, tab2_words[a]) for a in range(2)]
+        load_scale_rows(w_s_raw[:, 0:H], w2_scales)
+        load_scale_rows(w_s_raw[:, H : 2 * H], w3_scales)
+        w2_raw = held("w2_raw", [P, 2, H], I32)
+        nc.sync.dma_start(w2_raw[:], w2_words.rearrange("a p n i -> p a (n i)").bitcast(I32))
+        w3_raw = held("w3_raw", [P, H // 2], I32)
+        nc.sync.dma_start(w3_raw[:], w3_words[0].bitcast(I32))
+        tab3_w = load_words("tab3_w", tab3_words[0])
+        p1 = load_list("p1", pos1)
+        p2 = load_list("p2", pos2)
+        p3 = load_list("p3", pos3)
+        cap_t = held("cap_t", [P, 2, 16], F32)
+        cap_runs = cap.rearrange("(b h x) -> h b x", b=2, x=16)
+        for i in range(4):
+            nc.sync.dma_start(cap_t[i:P:4, :, 0:13], cap_runs[:, :, i : i + 13])
+
+        def gather_words(name, window, offsets):
+            dst = held(name, [P, S], U32)
+            nc.vector.tensor_copy(dst[:], window[:].bitcast(U32).indirect(offsets[:]))
+            return dst
+
+        def gather_scales(name, window, offsets):
+            dst = held(name, [P, S], U8)
+            nc.vector.tensor_copy(dst[:], window[:].indirect(offsets[:]))
+            return dst
+
+        def quantize(name, grouped):
+            cols = grouped.shape[1] // 4
+            codes = held(name + "_codes", [P, cols], U32)
+            scales = held(name + "_scales", [P, cols], U8)
+            nc.vector.quantize_mx(out=codes[:].bitcast(FP8X4), scales=scales[:], in_=grouped)
+            return codes, scales
+
+        v_s = gather_scales("v_s", tab_s, idx)
+        v_w = gather_words("v_w", tab_w, idx)
+        v2_s = gather_scales("v2_s", tab2_s, idx2)
+        v3_s = gather_scales("v3_s", tab3_s, idx3)
+
+        w1_q = []
+        for b in range(2):
+            grouped = keep.tile([P, 4 * BANK], BF16, name="w1_bf", tag="w_bf", bufs=2, align_bytes=64)
+            by_slice = w1_raw[b][:].rearrange("p j (h t i) -> p t h j i", t=4, i=4)
+            for t in range(4):
+                nc.scalar.activation(
+                    grouped[:, BANK * t : BANK * (t + 1)].rearrange("p (h i j) -> p h j i", i=4, j=4),
+                    by_slice[:, t], ACT.Copy,
+                )
+            w1_q.append(quantize("w1_%d" % b, grouped[:]))
+
+        v2_w = [gather_words("v2_w%d" % a, tab2_w[a], idx2) for a in range(2)]
+
+        w_s = held("w_s", [P, 2 * H], U8)
+        nc.vector.tensor_copy(
+            w_s[:].bitcast(I32).rearrange("p (x t h) -> p x t h", x=4, t=4),
+            w_s_raw[:].bitcast(I32).rearrange("p (x h t) -> p x t h", x=4, t=4),
+        )
+        w2_w = held("w2_w", [P, 2 * H], I32)
+        nc.vector.tensor_copy(
+            w2_w[:].rearrange("p (x t h i) -> p x t h i", x=4, t=4, i=4),
+            w2_raw[:].rearrange("p a (b h t i) -> p (a b) t h i", b=2, t=4, i=4),
+        )
+        v3_w = gather_words("v3_w", tab3_w, idx3)
+        w3_w = held("w3_w", [P, 2 * H], U8)
+        nc.vector.tensor_copy(
+            w3_w[:].bitcast(I32).rearrange("p (b t h i) -> p b t h i", b=2, t=4, i=2),
+            w3_raw[:].rearrange("p (b h t i) -> p b t h i", b=2, t=4, i=2),
+        )
+
+        def first_stage(passes):
+            rows = keep.tile([P, S], F32, name="rows", tag="rows", bufs=16, align_bytes=64)
+            for half in range(2):
+                cols = slice(BANK * half, BANK * (half + 1))
+                acc = psum.tile([P, BANK], F32, name="acc", tag="ring", bufs=6)
+                for n, (lhs, lhs_s, rhs, rhs_s) in enumerate(passes):
+                    nc.tensor.matmul_mx(
+                        out=acc[:], lhsT=lhs, lhsT_scale=lhs_s,
+                        rhs=rhs[:, cols].bitcast(FP8X4), rhs_scale=rhs_s[:, cols],
+                        start=(n == 0), stop=(n == len(passes) - 1),
+                    )
+                nc.scalar.copy(rows[:, cols], acc[:])
+            return rows
+
+        def a_slice(s):
+            codes, scales = w1_q[s // 4]
+            cols = slice(P * (s % 4), P * (s % 4 + 1))
+            return first_stage([(codes[:, cols].bitcast(FP8X4), scales[:, cols], v_w, v_s)])
+
+        def b_slice(s):
+            return first_stage([
+                (
+                    w2_w[:, H * a + P * s : H * a + P * (s + 1)].bitcast(FP8X4),
+                    w_s[4 * a : P, P * s : P * (s + 1)],
+                    v2_w[a], v2_s[4 * a : P, :],
+                )
+                for a in range(2)
+            ])
+
+        def d_slice(s):
+            return first_stage([(
+                w3_w[:, 2 * P * s : 2 * P * (s + 1)].bitcast(FP4X4),
+                w_s[:, H + P * s : H + P * (s + 1)], v3_w, v3_s,
+            )])
+
+        a_rows = [a_slice(s) for s in range(8)]
+        a_picked = [
+            keep.tile([P, 4, J], F32, name="a_picked", tag="quad", bufs=2, align_bytes=64) for b in range(2)
+        ]
+        for s in range(8):
+            nc.vector.tensor_copy(a_picked[s // 4][:, s % 4, :], a_rows[s][:].indirect(p1[:]))
+
+        gaps = []
+        for s in range(8):
+            b_rows = b_slice(s)
+            gap = held("gap%d" % s, [P, J], F32)
+            nc.vector.tensor_tensor(gap[:], b_rows[:].indirect(p2[:]), a_picked[s // 4][:, s % 4, :], ALU.subtract)
+            gaps.append(gap)
+
+        def interleave(dst, src, scale):
+            nc.scalar.activation(
+                dst.rearrange("p (c i t) -> p c t i", i=4, t=4),
+                src.rearrange("p t (c i) -> p c t i", i=4),
+                ACT.Copy, scale=scale,
+            )
+
+        w4_q = []
+        for b in range(2):
+            raw = keep.tile([P, 4, N], F32, name="w4_raw", tag="w_raw", bufs=2, align_bytes=64)
+            by_slot = w4[BANK * b : BANK * (b + 1), :].rearrange("(h t i) n -> t h i n", t=4, i=4)
+            for t in range(4):
+                nc.sync.dma_start(raw[:, t, :], by_slot[t])
+            grouped = keep.tile([P, 4 * N], BF16, name="w4_bf", tag="w_bf", bufs=2, align_bytes=64)
+            interleave(grouped[:], raw[:], 1.0)
+            w4_q.append(quantize("w4_%d" % b, grouped[:]))
+        pref_t = held("pref_t", [P, 4, J], F32)
+        nc.sync.dma_start(pref_t[:], pref.rearrange("(c p) j -> p c j", p=P))
+
+        def cap_square(s):
+            nc.scalar.activation(gaps[s][:], gaps[s][:], ACT.Square)
+            nc.vector.tensor_scalar(gaps[s][:], gaps[s][:], cap_t[:, s // 4, 4 * (s % 4) : 4 * (s % 4) + 1], None, ALU.min)
+
+        neg_z = [
+            keep.tile([P, 4, J], F32, name="neg_z", tag="quad", bufs=2, align_bytes=64) for b in range(2)
+        ]
+        d_rows = []
+
+        def take_off_d(s, cols):
+            nc.vector.tensor_tensor(
+                neg_z[s // 4][:, s % 4, cols],
+                d_rows[s][:].indirect(p3[:, cols.start // 16 : cols.stop // 16]),
+                gaps[s][:, cols], ALU.subtract,
+            )
+
+        def quantize_z(name, b, cols):
+            grouped = held(name + "_bf", [P, 4 * (cols.stop - cols.start)], BF16)
+            interleave(grouped[:], neg_z[b][:, :, cols], -1.0)
+            return quantize(name, grouped[:])
+
+        cap_square(0)
+        for s in range(8):
+            if s + 1 < 8:
+                cap_square(s + 1)
+            d_rows.append(d_slice(s))
+            if s < 4:
+                take_off_d(s, slice(0, J))
+            if s == 3:
+                z0 = quantize_z("z0", 0, slice(0, J))
+
+        def last_pass(acc, c, b, z_q, cols):
+            n_cols = slice(P * c, P * (c + 1))
+            nc.tensor.matmul_mx(
+                out=acc, lhsT=w4_q[b][0][:, n_cols].bitcast(FP8X4), lhsT_scale=w4_q[b][1][:, n_cols],
+                rhs=z_q[0][:, cols].bitcast(FP8X4), rhs_scale=z_q[1][:, cols],
+                start=(b == 0), stop=(b == 1),
+            )
+
+        out_by_tile = out.rearrange("(c p) j -> p c j", p=P)
+        first, second, whole = slice(0, HALF), slice(HALF, J), slice(0, HALF)
+
+        for s in range(4, 8):
+            take_off_d(s, first)
+        z1_first = quantize_z("z1a", 1, first)
+        for s in range(4, 8):
+            take_off_d(s, second)
+
+        late = [psum.tile([P, HALF], F32, name="late", tag="ring", bufs=6) for c in range(4)]
+        for c in range(4):
+            last_pass(late[c][:], c, 0, z0, second)
+        for pair in range(2):
+            acc = psum.tile([P, 2, HALF], F32, name="early%d" % pair)
+            for c in range(2):
+                last_pass(acc[:, c, :], 2 * pair + c, 0, z0, first)
+                last_pass(acc[:, c, :], 2 * pair + c, 1, z1_first, whole)
+            tiles = slice(2 * pair, 2 * pair + 2)
+            nc.vector.tensor_tensor(pref_t[:, tiles, first], acc[:], pref_t[:, tiles, first], ALU.add)
+            nc.sync.dma_start(out_by_tile[:, tiles, first], pref_t[:, tiles, first])
+
+        z1_second = quantize_z("z1b", 1, second)
+        for c in range(4):
+            last_pass(late[c][:], c, 1, z1_second, whole)
+            nc.vector.tensor_tensor(pref_t[:, c, second], late[c][:], pref_t[:, c, second], ALU.add)
+            nc.sync.dma_start(out_by_tile[:, c, second], pref_t[:, c, second])

@@ -39,10 +39,10 @@ def tile_list_key_blank_bench_kernel(
             nc.sync.dma_start(dst[:], src)
             return dst
 
-        def load_scale_rows(dst, src):
+        def load_scale_rows(dst, src, queue=nc.sync):
             rows = 4 * src.shape[0]
             for q in range(4):
-                nc.sync.dma_start(dst[32 * q : 32 * q + rows, :].bitcast(I32), src[:, 4 * q : 4 * q + 4, :].bitcast(I32))
+                queue.dma_start(dst[32 * q : 32 * q + rows, :].bitcast(I32), src[:, 4 * q : 4 * q + 4, :].bitcast(I32))
 
         def load_words(name, src):
             dst = held(name, [P, T], I32)
@@ -57,10 +57,10 @@ def tile_list_key_blank_bench_kernel(
             nc.vector.memset(plane[:].bitcast(I32), 0)
 
         idx = load_list("idx", offs)
+        load_scale_rows(tab_s, tab_scales, nc.scalar)
+        tab_w = load_words("tab_w", tab_words[0])
         idx2 = load_list("idx2", offs2)
         idx3 = load_list("idx3", offs3)
-        load_scale_rows(tab_s, tab_scales)
-        tab_w = load_words("tab_w", tab_words[0])
         load_scale_rows(tab2_s, tab2_scales)
         w1_raw = []
         for b in range(2):
@@ -109,12 +109,19 @@ def tile_list_key_blank_bench_kernel(
         w1_q = []
         for b in range(2):
             grouped = keep.tile([P, 4 * BANK], BF16, name="w1_bf", tag="w_bf", bufs=2, align_bytes=64)
-            by_slice = w1_raw[b][:].rearrange("p j (h t i) -> p t h j i", t=4, i=4)
             for t in range(4):
-                nc.scalar.activation(
-                    grouped[:, BANK * t : BANK * (t + 1)].rearrange("p (h i j) -> p h j i", i=4, j=4),
-                    by_slice[:, t], ACT.Copy,
-                )
+                dst = grouped[:, BANK * t : BANK * (t + 1)]
+                if b == 0:
+                    nc.scalar.activation(
+                        dst.rearrange("p (h i j) -> p h j i", i=4, j=4),
+                        w1_raw[b][:].rearrange("p j (h t i) -> p t h j i", t=4, i=4)[:, t], ACT.Copy,
+                    )
+                else:
+                    nc.gpsimd.tensor_scalar(
+                        dst.rearrange("p (h i j) -> p h i j", i=4, j=4),
+                        w1_raw[b][:].rearrange("p j (h t i) -> p t h i j", t=4, i=4)[:, t],
+                        1.0, 0.0, ALU.mult, ALU.add,
+                    )
             w1_q.append(quantize("w1_%d" % b, grouped[:]))
 
         v2_w = [gather_words("v2_w%d" % a, tab2_w[a], idx2) for a in range(2)]
@@ -140,7 +147,7 @@ def tile_list_key_blank_bench_kernel(
             rows = keep.tile([P, S], F32, name="rows", tag="rows", bufs=16, align_bytes=64)
             for half in range(2):
                 cols = slice(BANK * half, BANK * (half + 1))
-                acc = psum.tile([P, BANK], F32, name="acc", tag="ring", bufs=6)
+                acc = psum.tile([P, BANK], F32, name="acc", tag="ring", bufs=8)
                 for n, (lhs, lhs_s, rhs, rhs_s) in enumerate(passes):
                     nc.tensor.matmul_mx(
                         out=acc[:], lhsT=lhs, lhsT_scale=lhs_s,
@@ -199,7 +206,12 @@ def tile_list_key_blank_bench_kernel(
             for t in range(4):
                 nc.sync.dma_start(raw[:, t, :], by_slot[t])
             grouped = keep.tile([P, 4 * N], BF16, name="w4_bf", tag="w_bf", bufs=2, align_bytes=64)
-            interleave(grouped[:], raw[:], 1.0)
+            for half in range(2):
+                nc.gpsimd.tensor_scalar(
+                    grouped[:, 4 * HALF * half : 4 * HALF * (half + 1)].rearrange("p (n t) -> p n t", t=4),
+                    raw[:, :, HALF * half : HALF * (half + 1)].rearrange("p t n -> p n t"),
+                    1.0, 0.0, ALU.mult, ALU.add,
+                )
             w4_q.append(quantize("w4_%d" % b, grouped[:]))
         pref_t = held("pref_t", [P, 4, J], F32)
         nc.sync.dma_start(pref_t[:], pref.rearrange("(c p) j -> p c j", p=P))
@@ -208,64 +220,62 @@ def tile_list_key_blank_bench_kernel(
             nc.scalar.activation(gaps[s][:], gaps[s][:], ACT.Square)
             nc.vector.tensor_scalar(gaps[s][:], gaps[s][:], cap_t[:, s // 4, 4 * (s % 4) : 4 * (s % 4) + 1], None, ALU.min)
 
-        neg_z = [
-            keep.tile([P, 4, J], F32, name="neg_z", tag="quad", bufs=2, align_bytes=64) for b in range(2)
-        ]
         d_rows = []
 
-        def take_off_d(s, cols):
+        def take_off_d(s, dst, cols):
             nc.vector.tensor_tensor(
-                neg_z[s // 4][:, s % 4, cols],
-                d_rows[s][:].indirect(p3[:, cols.start // 16 : cols.stop // 16]),
+                dst[:, s % 4, :], d_rows[s][:].indirect(p3[:, cols.start // 16 : cols.stop // 16]),
                 gaps[s][:, cols], ALU.subtract,
             )
 
-        def quantize_z(name, b, cols):
-            grouped = held(name + "_bf", [P, 4 * (cols.stop - cols.start)], BF16)
-            interleave(grouped[:], neg_z[b][:, :, cols], -1.0)
+        def quantize_z(name, neg_z, tag):
+            grouped = keep.tile([P, 4 * neg_z.shape[2]], BF16, name=name + "_bf", tag=tag, align_bytes=64)
+            interleave(grouped[:], neg_z[:], -1.0)
             return quantize(name, grouped[:])
 
+        neg_z0 = keep.tile([P, 4, J], F32, name="neg_z0", tag="quad", bufs=2, align_bytes=64)
         cap_square(0)
         for s in range(8):
             if s + 1 < 8:
                 cap_square(s + 1)
             d_rows.append(d_slice(s))
             if s < 4:
-                take_off_d(s, slice(0, J))
-            if s == 3:
-                z0 = quantize_z("z0", 0, slice(0, J))
+                take_off_d(s, neg_z0, slice(0, J))
 
-        def last_pass(acc, c, b, z_q, cols):
-            n_cols = slice(P * c, P * (c + 1))
-            nc.tensor.matmul_mx(
-                out=acc, lhsT=w4_q[b][0][:, n_cols].bitcast(FP8X4), lhsT_scale=w4_q[b][1][:, n_cols],
-                rhs=z_q[0][:, cols].bitcast(FP8X4), rhs_scale=z_q[1][:, cols],
-                start=(b == 0), stop=(b == 1),
-            )
+        def piece_of_neg_z1(cols, tag, bufs=1):
+            neg_z1 = keep.tile([P, 4, cols.stop - cols.start], F32, name="neg_z1", tag=tag, bufs=bufs, align_bytes=64)
+            for s in range(4, 8):
+                take_off_d(s, neg_z1, cols)
+            return neg_z1
 
         out_by_tile = out.rearrange("(c p) j -> p c j", p=P)
-        first, second, whole = slice(0, HALF), slice(HALF, J), slice(0, HALF)
 
-        for s in range(4, 8):
-            take_off_d(s, first)
-        z1_first = quantize_z("z1a", 1, first)
-        for s in range(4, 8):
-            take_off_d(s, second)
+        def finish(cols, z1):
+            width = cols.stop - cols.start
+            per_bank = BANK // width
+            for first in range(0, 4, per_bank):
+                acc = psum.tile([P, per_bank, width], F32, name="y", tag="ring", bufs=8)
+                for c in range(per_bank):
+                    n_cols = slice(P * (first + c), P * (first + c + 1))
+                    for b, (z_q, z_cols) in enumerate([(z0, cols), (z1, slice(0, width))]):
+                        nc.tensor.matmul_mx(
+                            out=acc[:, c, :],
+                            lhsT=w4_q[b][0][:, n_cols].bitcast(FP8X4), lhsT_scale=w4_q[b][1][:, n_cols],
+                            rhs=z_q[0][:, z_cols].bitcast(FP8X4), rhs_scale=z_q[1][:, z_cols],
+                            start=(b == 0), stop=(b == 1),
+                        )
+                tiles = slice(first, first + per_bank)
+                nc.vector.tensor_tensor(pref_t[:, tiles, cols], acc[:], pref_t[:, tiles, cols], ALU.add)
+                nc.sync.dma_start(out_by_tile[:, tiles, cols], pref_t[:, tiles, cols])
 
-        late = [psum.tile([P, HALF], F32, name="late", tag="ring", bufs=6) for c in range(4)]
-        for c in range(4):
-            last_pass(late[c][:], c, 0, z0, second)
-        for pair in range(2):
-            acc = psum.tile([P, 2, HALF], F32, name="early%d" % pair)
-            for c in range(2):
-                last_pass(acc[:, c, :], 2 * pair + c, 0, z0, first)
-                last_pass(acc[:, c, :], 2 * pair + c, 1, z1_first, whole)
-            tiles = slice(2 * pair, 2 * pair + 2)
-            nc.vector.tensor_tensor(pref_t[:, tiles, first], acc[:], pref_t[:, tiles, first], ALU.add)
-            nc.sync.dma_start(out_by_tile[:, tiles, first], pref_t[:, tiles, first])
-
-        z1_second = quantize_z("z1b", 1, second)
-        for c in range(4):
-            last_pass(late[c][:], c, 1, z1_second, whole)
-            nc.vector.tensor_tensor(pref_t[:, c, second], late[c][:], pref_t[:, c, second], ALU.add)
-            nc.sync.dma_start(out_by_tile[:, c, second], pref_t[:, c, second])
+        pieces = [slice(0, 256), slice(256, 384), slice(384, 512)]
+        neg_a = piece_of_neg_z1(pieces[0], "quad", 2)
+        neg_b = piece_of_neg_z1(pieces[1], "neg_b")
+        z0 = quantize_z("z0", neg_z0, "z0_bf")
+        z1_a = quantize_z("z1a", neg_a, "shared")
+        neg_c = piece_of_neg_z1(pieces[2], "shared")
+        z1_b = quantize_z("z1b", neg_b, "z1b_bf")
+        finish(pieces[0], z1_a)
+        z1_c = quantize_z("z1c", neg_c, "z1c_bf")
+        finish(pieces[1], z1_b)
+        finish(pieces[2], z1_c)

@@ -56,33 +56,30 @@ def tile_list_key_blank_bench_kernel(
         for plane in (tab_s, tab2_s, tab3_s, w_s_raw):
             nc.vector.memset(plane[:].bitcast(I32), 0)
 
+        def load_w1(b):
+            raw = keep.tile([P, 4, BANK], F32, name="w1_raw", tag="w_raw", bufs=2, align_bytes=64)
+            nc.sync.dma_start(raw[:], w1[:, BANK * b : BANK * (b + 1)].rearrange("(p j) c -> p j c", j=4))
+            return raw
+
         idx = load_list("idx", offs)
         load_scale_rows(tab_s, tab_scales, nc.scalar)
         tab_w = load_words("tab_w", tab_words[0])
+        w1_raw = [load_w1(0)]
         idx2 = load_list("idx2", offs2)
-        idx3 = load_list("idx3", offs3)
         load_scale_rows(tab2_s, tab2_scales)
-        w1_raw = []
-        for b in range(2):
-            raw = keep.tile([P, 4, BANK], F32, name="w1_raw", tag="w_raw", bufs=2, align_bytes=64)
-            nc.sync.dma_start(raw[:], w1[:, BANK * b : BANK * (b + 1)].rearrange("(p j) c -> p j c", j=4))
-            w1_raw.append(raw)
+        tab2_w = [load_words("tab2_w0", tab2_words[0])]
+        idx3 = load_list("idx3", offs3)
         load_scale_rows(tab3_s, tab3_scales)
-        tab2_w = [load_words("tab2_w%d" % a, tab2_words[a]) for a in range(2)]
+        w1_raw.append(load_w1(1))
         load_scale_rows(w_s_raw[:, 0:H], w2_scales)
+        tab2_w.append(load_words("tab2_w1", tab2_words[1]))
         load_scale_rows(w_s_raw[:, H : 2 * H], w3_scales)
-        w2_raw = held("w2_raw", [P, 2, H], I32)
-        nc.sync.dma_start(w2_raw[:], w2_words.rearrange("a p n i -> p a (n i)").bitcast(I32))
         w3_raw = held("w3_raw", [P, H // 2], I32)
         nc.sync.dma_start(w3_raw[:], w3_words[0].bitcast(I32))
-        tab3_w = load_words("tab3_w", tab3_words[0])
+        w2_raw = keep.tile([P, 2, H], I32, name="w2_raw", tag="w2_then_pref", align_bytes=64)
+        nc.sync.dma_start(w2_raw[:], w2_words.rearrange("a p n i -> p a (n i)").bitcast(I32))
         p1 = load_list("p1", pos1)
         p2 = load_list("p2", pos2)
-        p3 = load_list("p3", pos3)
-        cap_t = held("cap_t", [P, 2, 16], F32)
-        cap_runs = cap.rearrange("(b h x) -> h b x", b=2, x=16)
-        for i in range(4):
-            nc.sync.dma_start(cap_t[i:P:4, :, 0:13], cap_runs[:, :, i : i + 13])
 
         def gather_words(name, window, offsets):
             dst = held(name, [P, S], U32)
@@ -113,8 +110,8 @@ def tile_list_key_blank_bench_kernel(
                 dst = grouped[:, BANK * t : BANK * (t + 1)]
                 if b == 0:
                     nc.scalar.activation(
-                        dst.rearrange("p (h i j) -> p h j i", i=4, j=4),
-                        w1_raw[b][:].rearrange("p j (h t i) -> p t h j i", t=4, i=4)[:, t], ACT.Copy,
+                        dst.rearrange("p (h i j) -> p h i j", i=4, j=4),
+                        w1_raw[b][:].rearrange("p j (h t i) -> p t h i j", t=4, i=4)[:, t], ACT.Copy,
                     )
                 else:
                     nc.gpsimd.tensor_scalar(
@@ -136,12 +133,36 @@ def tile_list_key_blank_bench_kernel(
             w2_w[:].rearrange("p (x t h i) -> p x t h i", x=4, t=4, i=4),
             w2_raw[:].rearrange("p a (b h t i) -> p (a b) t h i", b=2, t=4, i=4),
         )
-        v3_w = gather_words("v3_w", tab3_w, idx3)
         w3_w = held("w3_w", [P, 2 * H], U8)
         nc.vector.tensor_copy(
             w3_w[:].bitcast(I32).rearrange("p (b t h i) -> p b t h i", b=2, t=4, i=2),
             w3_raw[:].rearrange("p (b h t i) -> p b t h i", b=2, t=4, i=2),
         )
+
+        w4_q = []
+        for b in range(2):
+            raw = keep.tile([P, 4, N], F32, name="w4_raw", tag="w_raw", bufs=2, align_bytes=64)
+            by_slot = w4[BANK * b : BANK * (b + 1), :].rearrange("(h t i) n -> t h i n", t=4, i=4)
+            for t in range(4):
+                nc.sync.dma_start(raw[:, t, :], by_slot[t])
+            grouped = keep.tile([P, 4 * N], BF16, name="w4_bf", tag="w_bf", bufs=2, align_bytes=64)
+            for c in range(4):
+                nc.gpsimd.tensor_scalar(
+                    grouped[:, 4 * P * c : 4 * P * (c + 1)].rearrange("p (n t) -> p n t", t=4),
+                    raw[:, :, P * c : P * (c + 1)].rearrange("p t n -> p n t"),
+                    1.0, 0.0, ALU.mult, ALU.add,
+                )
+            w4_q.append(quantize("w4_%d" % b, grouped[:]))
+
+        tab3_w = load_words("tab3_w", tab3_words[0])
+        p3 = load_list("p3", pos3)
+        cap_t = held("cap_t", [P, 2, 16], F32)
+        cap_runs = cap.rearrange("(b h x) -> h b x", b=2, x=16)
+        for i in range(4):
+            nc.sync.dma_start(cap_t[i:P:4, :, 0:13], cap_runs[:, :, i : i + 13])
+        pref_t = keep.tile([P, 4, J], F32, name="pref_t", tag="w2_then_pref", align_bytes=64)
+        nc.sync.dma_start(pref_t[:], pref.rearrange("(c p) j -> p c j", p=P))
+        v3_w = gather_words("v3_w", tab3_w, idx3)
 
         def first_stage(passes):
             rows = keep.tile([P, S], F32, name="rows", tag="rows", bufs=16, align_bytes=64)
@@ -194,27 +215,10 @@ def tile_list_key_blank_bench_kernel(
 
         def interleave(dst, src, scale):
             nc.scalar.activation(
-                dst.rearrange("p (c i t) -> p c t i", i=4, t=4),
-                src.rearrange("p t (c i) -> p c t i", i=4),
+                dst.rearrange("p (c t) -> p c t", t=4),
+                src.rearrange("p t c -> p c t"),
                 ACT.Copy, scale=scale,
             )
-
-        w4_q = []
-        for b in range(2):
-            raw = keep.tile([P, 4, N], F32, name="w4_raw", tag="w_raw", bufs=2, align_bytes=64)
-            by_slot = w4[BANK * b : BANK * (b + 1), :].rearrange("(h t i) n -> t h i n", t=4, i=4)
-            for t in range(4):
-                nc.sync.dma_start(raw[:, t, :], by_slot[t])
-            grouped = keep.tile([P, 4 * N], BF16, name="w4_bf", tag="w_bf", bufs=2, align_bytes=64)
-            for half in range(2):
-                nc.gpsimd.tensor_scalar(
-                    grouped[:, 4 * HALF * half : 4 * HALF * (half + 1)].rearrange("p (n t) -> p n t", t=4),
-                    raw[:, :, HALF * half : HALF * (half + 1)].rearrange("p t n -> p n t"),
-                    1.0, 0.0, ALU.mult, ALU.add,
-                )
-            w4_q.append(quantize("w4_%d" % b, grouped[:]))
-        pref_t = held("pref_t", [P, 4, J], F32)
-        nc.sync.dma_start(pref_t[:], pref.rearrange("(c p) j -> p c j", p=P))
 
         def cap_square(s):
             nc.scalar.activation(gaps[s][:], gaps[s][:], ACT.Square)
@@ -250,9 +254,8 @@ def tile_list_key_blank_bench_kernel(
 
         out_by_tile = out.rearrange("(c p) j -> p c j", p=P)
 
-        def finish(cols, z1):
+        def finish(cols, z1, per_bank):
             width = cols.stop - cols.start
-            per_bank = BANK // width
             for first in range(0, 4, per_bank):
                 acc = psum.tile([P, per_bank, width], F32, name="y", tag="ring", bufs=8)
                 for c in range(per_bank):
@@ -275,7 +278,7 @@ def tile_list_key_blank_bench_kernel(
         z1_a = quantize_z("z1a", neg_a, "shared")
         neg_c = piece_of_neg_z1(pieces[2], "shared")
         z1_b = quantize_z("z1b", neg_b, "z1b_bf")
-        finish(pieces[0], z1_a)
+        finish(pieces[0], z1_a, 2)
         z1_c = quantize_z("z1c", neg_c, "z1c_bf")
-        finish(pieces[1], z1_b)
-        finish(pieces[2], z1_c)
+        finish(pieces[1], z1_b, 4)
+        finish(pieces[2], z1_c, 2)

@@ -79,6 +79,7 @@ def tile_list_key_blank_bench_kernel(
         w2_raw = keep.tile([P, 2, H], I32, name="w2_raw", tag="w2_then_pref", align_bytes=64)
         nc.sync.dma_start(w2_raw[:], w2_words.rearrange("a p n i -> p a (n i)").bitcast(I32))
         p1 = load_list("p1", pos1)
+        tab3_w = load_words("tab3_w", tab3_words[0])
         p2 = load_list("p2", pos2)
 
         def gather_words(name, window, offsets):
@@ -110,8 +111,8 @@ def tile_list_key_blank_bench_kernel(
                 dst = grouped[:, BANK * t : BANK * (t + 1)]
                 if b == 0:
                     nc.scalar.activation(
-                        dst.rearrange("p (h i j) -> p h i j", i=4, j=4),
-                        w1_raw[b][:].rearrange("p j (h t i) -> p t h i j", t=4, i=4)[:, t], ACT.Copy,
+                        dst.rearrange("p (h i j) -> p h j i", i=4, j=4),
+                        w1_raw[b][:].rearrange("p j (h t i) -> p t h j i", t=4, i=4)[:, t], ACT.Copy,
                     )
                 else:
                     nc.gpsimd.tensor_scalar(
@@ -128,7 +129,7 @@ def tile_list_key_blank_bench_kernel(
             w_s[:].bitcast(I32).rearrange("p (x t h) -> p x t h", x=4, t=4),
             w_s_raw[:].bitcast(I32).rearrange("p (x h t) -> p x t h", x=4, t=4),
         )
-        w2_w = held("w2_w", [P, 2 * H], I32)
+        w2_w = keep.tile([P, 2 * H], I32, name="w2_w", tag="w2_then_gaps", align_bytes=64)
         nc.vector.tensor_copy(
             w2_w[:].rearrange("p (x t h i) -> p x t h i", x=4, t=4, i=4),
             w2_raw[:].rearrange("p a (b h t i) -> p (a b) t h i", b=2, t=4, i=4),
@@ -138,6 +139,8 @@ def tile_list_key_blank_bench_kernel(
             w3_w[:].bitcast(I32).rearrange("p (b t h i) -> p b t h i", b=2, t=4, i=2),
             w3_raw[:].rearrange("p (b h t i) -> p b t h i", b=2, t=4, i=2),
         )
+
+        v3_w = gather_words("v3_w", tab3_w, idx3)
 
         w4_q = []
         for b in range(2):
@@ -154,7 +157,6 @@ def tile_list_key_blank_bench_kernel(
                 )
             w4_q.append(quantize("w4_%d" % b, grouped[:]))
 
-        tab3_w = load_words("tab3_w", tab3_words[0])
         p3 = load_list("p3", pos3)
         cap_t = held("cap_t", [P, 2, 16], F32)
         cap_runs = cap.rearrange("(b h x) -> h b x", b=2, x=16)
@@ -162,10 +164,9 @@ def tile_list_key_blank_bench_kernel(
             nc.sync.dma_start(cap_t[i:P:4, :, 0:13], cap_runs[:, :, i : i + 13])
         pref_t = keep.tile([P, 4, J], F32, name="pref_t", tag="w2_then_pref", align_bytes=64)
         nc.sync.dma_start(pref_t[:], pref.rearrange("(c p) j -> p c j", p=P))
-        v3_w = gather_words("v3_w", tab3_w, idx3)
 
-        def first_stage(passes):
-            rows = keep.tile([P, S], F32, name="rows", tag="rows", bufs=16, align_bytes=64)
+        def first_stage(passes, tag="rows", bufs=16):
+            rows = keep.tile([P, S], F32, name="rows", tag=tag, bufs=bufs, align_bytes=64)
             for half in range(2):
                 cols = slice(BANK * half, BANK * (half + 1))
                 acc = psum.tile([P, BANK], F32, name="acc", tag="ring", bufs=8)
@@ -193,11 +194,11 @@ def tile_list_key_blank_bench_kernel(
                 for a in range(2)
             ])
 
-        def d_slice(s):
+        def d_slice(s, *place):
             return first_stage([(
                 w3_w[:, 2 * P * s : 2 * P * (s + 1)].bitcast(FP4X4),
                 w_s[:, H + P * s : H + P * (s + 1)], v3_w, v3_s,
-            )])
+            )], *place)
 
         a_rows = [a_slice(s) for s in range(8)]
         a_picked = [
@@ -206,25 +207,24 @@ def tile_list_key_blank_bench_kernel(
         for s in range(8):
             nc.vector.tensor_copy(a_picked[s // 4][:, s % 4, :], a_rows[s][:].indirect(p1[:]))
 
-        gaps = []
+        b_rows = [b_slice(s) for s in range(8)]
+        all_gaps = keep.tile([P, 8 * J], F32, name="all_gaps", tag="w2_then_gaps", align_bytes=64)
+        gaps = [all_gaps[:, J * s : J * (s + 1)] for s in range(8)]
         for s in range(8):
-            b_rows = b_slice(s)
-            gap = held("gap%d" % s, [P, J], F32)
-            nc.vector.tensor_tensor(gap[:], b_rows[:].indirect(p2[:]), a_picked[s // 4][:, s % 4, :], ALU.subtract)
-            gaps.append(gap)
+            nc.vector.tensor_tensor(gaps[s], b_rows[s][:].indirect(p2[:]), a_picked[s // 4][:, s % 4, :], ALU.subtract)
 
         def interleave(dst, src, scale):
             nc.scalar.activation(
-                dst.rearrange("p (c t) -> p c t", t=4),
-                src.rearrange("p t c -> p c t"),
+                dst.rearrange("p (c i t) -> p c t i", i=4, t=4),
+                src.rearrange("p t (c i) -> p c t i", i=4),
                 ACT.Copy, scale=scale,
             )
 
         def cap_square(s):
-            nc.scalar.activation(gaps[s][:], gaps[s][:], ACT.Square)
-            nc.vector.tensor_scalar(gaps[s][:], gaps[s][:], cap_t[:, s // 4, 4 * (s % 4) : 4 * (s % 4) + 1], None, ALU.min)
+            nc.scalar.activation(gaps[s], gaps[s], ACT.Square)
+            nc.vector.tensor_scalar(gaps[s], gaps[s], cap_t[:, s // 4, 4 * (s % 4) : 4 * (s % 4) + 1], None, ALU.min)
 
-        d_rows = []
+        d_rows = {}
 
         def take_off_d(s, dst, cols):
             nc.vector.tensor_tensor(
@@ -234,20 +234,23 @@ def tile_list_key_blank_bench_kernel(
 
         def quantize_z(name, neg_z, tag):
             grouped = keep.tile([P, 4 * neg_z.shape[2]], BF16, name=name + "_bf", tag=tag, align_bytes=64)
-            interleave(grouped[:], neg_z[:], -1.0)
+            interleave(grouped[:], neg_z, -1.0)
             return quantize(name, grouped[:])
 
         neg_z0 = keep.tile([P, 4, J], F32, name="neg_z0", tag="quad", bufs=2, align_bytes=64)
+        for s in range(4, 8):
+            d_rows[s] = d_slice(s)
         cap_square(0)
-        for s in range(8):
-            if s + 1 < 8:
-                cap_square(s + 1)
-            d_rows.append(d_slice(s))
-            if s < 4:
-                take_off_d(s, neg_z0, slice(0, J))
+        for s in range(3):
+            cap_square(s + 1)
+            d_rows[s] = d_slice(s)
+            take_off_d(s, neg_z0, slice(0, J))
+        for s in range(4, 8):
+            cap_square(s)
+        d_rows[3] = d_slice(3, "d3_then_z1", 1)
+        take_off_d(3, neg_z0, slice(0, J))
 
-        def piece_of_neg_z1(cols, tag, bufs=1):
-            neg_z1 = keep.tile([P, 4, cols.stop - cols.start], F32, name="neg_z1", tag=tag, bufs=bufs, align_bytes=64)
+        def piece_of_neg_z1(neg_z1, cols):
             for s in range(4, 8):
                 take_off_d(s, neg_z1, cols)
             return neg_z1
@@ -272,13 +275,15 @@ def tile_list_key_blank_bench_kernel(
                 nc.sync.dma_start(out_by_tile[:, tiles, cols], pref_t[:, tiles, cols])
 
         pieces = [slice(0, 256), slice(256, 384), slice(384, 512)]
-        neg_a = piece_of_neg_z1(pieces[0], "quad", 2)
-        neg_b = piece_of_neg_z1(pieces[1], "neg_b")
-        z0 = quantize_z("z0", neg_z0, "z0_bf")
+        neg_ab = keep.tile([P, 4 * 384], F32, name="neg_ab", tag="d3_then_z1", align_bytes=64)
+        neg_a = piece_of_neg_z1(neg_ab[:, 0:1024].rearrange("p (t j) -> p t j", t=4), pieces[0])
+        neg_b = piece_of_neg_z1(neg_ab[:, 1024:1536].rearrange("p (t j) -> p t j", t=4), pieces[1])
+        z0 = quantize_z("z0", neg_z0[:], "z0_bf")
         z1_a = quantize_z("z1a", neg_a, "shared")
-        neg_c = piece_of_neg_z1(pieces[2], "shared")
+        neg_c = keep.tile([P, 4, 128], F32, name="neg_c", tag="shared", align_bytes=64)
+        piece_of_neg_z1(neg_c, pieces[2])
         z1_b = quantize_z("z1b", neg_b, "z1b_bf")
         finish(pieces[0], z1_a, 2)
-        z1_c = quantize_z("z1c", neg_c, "z1c_bf")
+        z1_c = quantize_z("z1c", neg_c[:], "z1c_bf")
         finish(pieces[1], z1_b, 4)
         finish(pieces[2], z1_c, 2)

from contextlib import ExitStack

import concourse.mybir as mybir

K, M, H, N, T, S, J = 512, 1024, 1024, 512, 2048, 1024, 512
FLOPS = 2 * H * S * (K + M + K) + 2 * H * N * J

F32 = mybir.dt.float32
BF16 = mybir.dt.bfloat16
I32 = mybir.dt.int32
U32 = mybir.dt.uint32
U16 = mybir.dt.uint16
U8 = mybir.dt.uint8
FP8X4 = mybir.dt.float8_e4m3fn_x4
FP4X4 = mybir.dt.float4_e2m1fn_x4
ACT = mybir.ActivationFunctionType
ALU = mybir.AluOpType

P = 128
BANK = 512
HALF = 256


def tile_list_key_blank_bench_kernel(
    tc, tab_words, tab_scales, tab2_words, tab2_scales, tab3_words, tab3_scales,
    offs, offs2, offs3, pos1, pos2, pos3,
    w1, w2_words, w2_scales, w3_words, w3_scales, cap, w4, pref, out,
):
    nc = tc.nc
    with ExitStack() as ctx:
        keep = ctx.enter_context(tc.tile_pool(name="keep", bufs=1))
        psum = ctx.enter_context(tc.psum_pool(name="psum", bufs=1))

        def held(name, shape, dtype):
            return keep.tile(shape, dtype, name=name, align_bytes=64)

        def load_list(name, src):
            dst = held(name, [P, src.shape[1]], U16)
            nc.sync.dma_start(dst[:], src)
            return dst

        def load_scale_rows(dst, src, queue=nc.sync):
            rows = 4 * src.shape[0]
            for q in range(4):
                queue.dma_start(dst[32 * q : 32 * q + rows, :].bitcast(I32), src[:, 4 * q : 4 * q + 4, :].bitcast(I32))

        def load_words(name, src):
            dst = held(name, [P, T], I32)
            nc.sync.dma_start(dst[:], src.rearrange("p n i -> p (n i)").bitcast(I32))
            return dst

        tab_s = held("tab_s", [P, T], U8)
        tab2_s = held("tab2_s", [P, T], U8)
        tab3_s = held("tab3_s", [P, T], U8)
        w_s_raw = held("w_s_raw", [P, 2 * H], U8)
        for plane in (tab_s, tab2_s, tab3_s, w_s_raw):
            nc.vector.memset(plane[:].bitcast(I32), 0)

        def load_w1(b):
            raw = keep.tile([P, 4, BANK], F32, name="w1_raw", tag="w_raw", bufs=2, align_bytes=64)
            nc.sync.dma_start(raw[:], w1[:, BANK * b : BANK * (b + 1)].rearrange("(p j) c -> p j c", j=4))
            return raw

        idx = load_list("idx", offs)
        load_scale_rows(tab_s, tab_scales, nc.scalar)
        tab_w = load_words("tab_w", tab_words[0])
        w1_raw = [load_w1(0)]
        idx2 = load_list("idx2", offs2)
        load_scale_rows(tab2_s, tab2_scales)
        tab2_w = [load_words("tab2_w0", tab2_words[0])]
        idx3 = load_list("idx3", offs3)
        load_scale_rows(tab3_s, tab3_scales)
        w1_raw.append(load_w1(1))
        load_scale_rows(w_s_raw[:, 0:H], w2_scales)
        tab2_w.append(load_words("tab2_w1", tab2_words[1]))
        load_scale_rows(w_s_raw[:, H : 2 * H], w3_scales)
        w3_raw = held("w3_raw", [P, H // 2], I32)
        nc.sync.dma_start(w3_raw[:], w3_words[0].bitcast(I32))
        w2_raw = keep.tile([P, 2, H], I32, name="w2_raw", tag="w2_then_pref", align_bytes=64)
        nc.sync.dma_start(w2_raw[:], w2_words.rearrange("a p n i -> p a (n i)").bitcast(I32))
        p1 = load_list("p1", pos1)
        tab3_w = load_words("tab3_w", tab3_words[0])
        p2 = load_list("p2", pos2)

        def gather_words(name, window, offsets):
            dst = held(name, [P, S], U32)
            nc.vector.tensor_copy(dst[:], window[:].bitcast(U32).indirect(offsets[:]))
            return dst

        def gather_scales(name, window, offsets):
            dst = held(name, [P, S], U8)
            nc.vector.tensor_copy(dst[:], window[:].indirect(offsets[:]))
            return dst

        def quantize(name, grouped):
            cols = grouped.shape[1] // 4
            codes = held(name + "_codes", [P, cols], U32)
            scales = held(name + "_scales", [P, cols], U8)
            nc.vector.quantize_mx(out=codes[:].bitcast(FP8X4), scales=scales[:], in_=grouped)
            return codes, scales

        v_s = gather_scales("v_s", tab_s, idx)
        v_w = gather_words("v_w", tab_w, idx)
        v2_s = gather_scales("v2_s", tab2_s, idx2)
        v3_s = gather_scales("v3_s", tab3_s, idx3)

        w1_q = []
        for b in range(2):
            grouped = keep.tile([P, 4 * BANK], BF16, name="w1_bf", tag="w_bf", bufs=2, align_bytes=64)
            for t in range(4):
                dst = grouped[:, BANK * t : BANK * (t + 1)]
                if b == 0:
                    nc.scalar.activation(
                        dst.rearrange("p (h i j) -> p h j i", i=4, j=4),
                        w1_raw[b][:].rearrange("p j (h t i) -> p t h j i", t=4, i=4)[:, t], ACT.Copy,
                    )
                else:
                    nc.gpsimd.tensor_scalar(
                        dst.rearrange("p (h i j) -> p h i j", i=4, j=4),
                        w1_raw[b][:].rearrange("p j (h t i) -> p t h i j", t=4, i=4)[:, t],
                        1.0, 0.0, ALU.mult, ALU.add,
                    )
            w1_q.append(quantize("w1_%d" % b, grouped[:]))

        v2_w = [gather_words("v2_w%d" % a, tab2_w[a], idx2) for a in range(2)]

        w_s = held("w_s", [P, 2 * H], U8)
        nc.vector.tensor_copy(
            w_s[:].bitcast(I32).rearrange("p (x t h) -> p x t h", x=4, t=4),
            w_s_raw[:].bitcast(I32).rearrange("p (x h t) -> p x t h", x=4, t=4),
        )
        w2_w = keep.tile([P, 2 * H], I32, name="w2_w", tag="w2_then_gaps", align_bytes=64)
        nc.vector.tensor_copy(
            w2_w[:].rearrange("p (x t h i) -> p x t h i", x=4, t=4, i=4),
            w2_raw[:].rearrange("p a (b h t i) -> p (a b) t h i", b=2, t=4, i=4),
        )
        w3_w = held("w3_w", [P, 2 * H], U8)
        nc.vector.tensor_copy(
            w3_w[:].bitcast(I32).rearrange("p (b t h i) -> p b t h i", b=2, t=4, i=2),
            w3_raw[:].rearrange("p (b h t i) -> p b t h i", b=2, t=4, i=2),
        )

        v3_w = gather_words("v3_w", tab3_w, idx3)

        w4_q = []
        for b in range(2):
            raw = keep.tile([P, 4, N], F32, name="w4_raw", tag="w_raw", bufs=2, align_bytes=64)
            by_slot = w4[BANK * b : BANK * (b + 1), :].rearrange("(h t i) n -> t h i n", t=4, i=4)
            for t in range(4):
                nc.sync.dma_start(raw[:, t, :], by_slot[t])
            grouped = keep.tile([P, 4 * N], BF16, name="w4_bf", tag="w_bf", bufs=2, align_bytes=64)
            for c in range(4):
                nc.gpsimd.tensor_scalar(
                    grouped[:, 4 * P * c : 4 * P * (c + 1)].rearrange("p (n t) -> p n t", t=4),
                    raw[:, :, P * c : P * (c + 1)].rearrange("p t n -> p n t"),
                    1.0, 0.0, ALU.mult, ALU.add,
                )
            w4_q.append(quantize("w4_%d" % b, grouped[:]))

        p3 = load_list("p3", pos3)
        cap_t = held("cap_t", [P, 2, 16], F32)
        cap_runs = cap.rearrange("(b h x) -> h b x", b=2, x=16)
        for i in range(4):
            nc.sync.dma_start(cap_t[i:P:4, :, 0:13], cap_runs[:, :, i : i + 13])
        pref_t = keep.tile([P, 4, J], F32, name="pref_t", tag="w2_then_pref", align_bytes=64)
        nc.sync.dma_start(pref_t[:], pref.rearrange("(c p) j -> p c j", p=P))

        def first_stage(passes, tag="rows", bufs=16):
            rows = keep.tile([P, S], F32, name="rows", tag=tag, bufs=bufs, align_bytes=64)
            for half in range(2):
                cols = slice(BANK * half, BANK * (half + 1))
                acc = psum.tile([P, BANK], F32, name="acc", tag="ring", bufs=8)
                for n, (lhs, lhs_s, rhs, rhs_s) in enumerate(passes):
                    nc.tensor.matmul_mx(
                        out=acc[:], lhsT=lhs, lhsT_scale=lhs_s,
                        rhs=rhs[:, cols].bitcast(FP8X4), rhs_scale=rhs_s[:, cols],
                        start=(n == 0), stop=(n == len(passes) - 1),
                    )
                nc.scalar.copy(rows[:, cols], acc[:])
            return rows

        def a_slice(s):
            codes, scales = w1_q[s // 4]
            cols = slice(P * (s % 4), P * (s % 4 + 1))
            return first_stage([(codes[:, cols].bitcast(FP8X4), scales[:, cols], v_w, v_s)])

        def b_slice(s):
            return first_stage([
                (
                    w2_w[:, H * a + P * s : H * a + P * (s + 1)].bitcast(FP8X4),
                    w_s[4 * a : P, P * s : P * (s + 1)],
                    v2_w[a], v2_s[4 * a : P, :],
                )
                for a in range(2)
            ])

        def d_slice(s, *place):
            return first_stage([(
                w3_w[:, 2 * P * s : 2 * P * (s + 1)].bitcast(FP4X4),
                w_s[:, H + P * s : H + P * (s + 1)], v3_w, v3_s,
            )], *place)

        a_rows = [a_slice(s) for s in range(8)]
        a_picked = [
            keep.tile([P, 4, J], F32, name="a_picked", tag="quad", bufs=2, align_bytes=64) for b in range(2)
        ]
        for s in range(8):
            nc.vector.tensor_copy(a_picked[s // 4][:, s % 4, :], a_rows[s][:].indirect(p1[:]))

        b_rows = [b_slice(s) for s in range(8)]
        all_gaps = keep.tile([P, 8 * J], F32, name="all_gaps", tag="w2_then_gaps", align_bytes=64)
        gaps = [all_gaps[:, J * s : J * (s + 1)] for s in range(8)]
        for s in range(8):
            nc.vector.tensor_tensor(gaps[s], b_rows[s][:].indirect(p2[:]), a_picked[s // 4][:, s % 4, :], ALU.subtract)

        def interleave(dst, src, scale):
            nc.scalar.activation(
                dst.rearrange("p (c i t) -> p c t i", i=4, t=4),
                src.rearrange("p t (c i) -> p c t i", i=4),
                ACT.Copy, scale=scale,
            )

        def cap_square(s):
            nc.scalar.activation(gaps[s], gaps[s], ACT.Square)
            nc.vector.tensor_scalar(gaps[s], gaps[s], cap_t[:, s // 4, 4 * (s % 4) : 4 * (s % 4) + 1], None, ALU.min)

        d_rows = {}

        def take_off_d(s, dst, cols):
            nc.vector.tensor_tensor(
                dst[:, s % 4, :], d_rows[s][:].indirect(p3[:, cols.start // 16 : cols.stop // 16]),
                gaps[s][:, cols], ALU.subtract,
            )

        def quantize_z(name, neg_z, tag):
            grouped = keep.tile([P, 4 * neg_z.shape[2]], BF16, name=name + "_bf", tag=tag, align_bytes=64)
            interleave(grouped[:], neg_z, -1.0)
            return quantize(name, grouped[:])

        neg_z0 = keep.tile([P, 4, J], F32, name="neg_z0", tag="quad", bufs=2, align_bytes=64)
        for s in range(4, 8):
            d_rows[s] = d_slice(s)
        cap_square(0)
        for s in range(3):
            cap_square(s + 1)
            d_rows[s] = d_slice(s)
            take_off_d(s, neg_z0, slice(0, J))
        for s in range(4, 8):
            cap_square(s)
        d_rows[3] = d_slice(3, "d3_then_z1", 1)
        take_off_d(3, neg_z0, slice(0, J))

        def piece_of_neg_z1(neg_z1, cols):
            for s in range(4, 8):
                take_off_d(s, neg_z1, cols)
            return neg_z1

        out_by_tile = out.rearrange("(c p) j -> p c j", p=P)

        def finish(cols, z1, per_bank):
            width = cols.stop - cols.start
            for first in range(0, 4, per_bank):
                acc = psum.tile([P, per_bank, width], F32, name="y", tag="ring", bufs=8)
                for c in range(per_bank):
                    n_cols = slice(P * (first + c), P * (first + c + 1))
                    for b, (z_q, z_cols) in enumerate([(z0, cols), (z1, slice(0, width))]):
                        nc.tensor.matmul_mx(
                            out=acc[:, c, :],
                            lhsT=w4_q[b][0][:, n_cols].bitcast(FP8X4), lhsT_scale=w4_q[b][1][:, n_cols],
                            rhs=z_q[0][:, z_cols].bitcast(FP8X4), rhs_scale=z_q[1][:, z_cols],
                            start=(b == 0), stop=(b == 1),
                        )
                tiles = slice(first, first + per_bank)
                nc.vector.tensor_tensor(pref_t[:, tiles, cols], acc[:], pref_t[:, tiles, cols], ALU.add)
                nc.sync.dma_start(out_by_tile[:, tiles, cols], pref_t[:, tiles, cols])

        pieces = [slice(0, 256), slice(256, 384), slice(384, 512)]
        neg_ab = keep.tile([P, 4 * 384], F32, name="neg_ab", tag="d3_then_z1", align_bytes=64)
        neg_a = piece_of_neg_z1(neg_ab[:, 0:1024].rearrange("p (t j) -> p t j", t=4), pieces[0])
        neg_b = piece_of_neg_z1(neg_ab[:, 1024:1536].rearrange("p (t j) -> p t j", t=4), pieces[1])
        z0 = quantize_z("z0", neg_z0[:], "z0_bf")
        z1_a = quantize_z("z1a", neg_a, "shared")
        neg_c = keep.tile([P, 4, 128], F32, name="neg_c", tag="shared", align_bytes=64)
        piece_of_neg_z1(neg_c, pieces[2])
        z1_b = quantize_z("z1b", neg_b, "z1b_bf")
        finish(pieces[0], z1_a, 2)
        z1_c = quantize_z("z1c", neg_c[:], "z1c_bf")
        finish(pieces[1], z1_b, 4)
        finish(pieces[2], z1_c, 2)
